import numpy as np
import ml_dtypes


def mxq(x, axis, fmt="e4m3"):
    dtype, down = {"e4m3": (ml_dtypes.float8_e4m3fn, 7), "e5m2": (ml_dtypes.float8_e5m2, 14)}[fmt]
    v = np.moveaxis(np.asarray(x, np.float32).astype(ml_dtypes.bfloat16).astype(np.float64), axis, -1)
    blocks = v.reshape(v.shape[:-1] + (-1, 32))
    amax = np.abs(blocks).max(-1, keepdims=True)
    byte = np.maximum(np.where(amax > 0, np.frexp(amax)[1] - 1 + 127, 0) - down, 1)
    scale = np.exp2(byte - 127.0)
    codes = (blocks / scale).astype(np.float32).astype(dtype).astype(np.float64)
    return np.moveaxis((codes * scale).reshape(v.shape), -1, axis)


WIDE = False


def mx_kscale(k):
    if not WIDE:
        return np.ones(k)
    levels = np.array([10, -10, 5, -5, 0])
    if k % 512:
        return np.exp2(np.random.permutation(np.resize(levels, k // 32))).repeat(32)
    a = np.empty((k // 512, 16))
    for p in range(k // 512):
        a[p, :8] = np.random.permutation(np.resize(levels, 8))
        for g in range(8):
            far = levels[np.abs(levels - a[p, g]) >= 10]
            a[p, g + 8] = far[np.random.randint(len(far))]
    return np.exp2(a.ravel()).repeat(32)


def f64(x):
    return np.asarray(x).astype(np.float64)


def striped8(idx):
    return np.asarray(idx).reshape(8, -1, 16).transpose(0, 2, 1).reshape(128, -1).astype(np.uint16)


def unstriped8(offs):
    return offs.reshape(8, 16, -1).transpose(0, 2, 1).reshape(8, -1).astype(np.int64)


def pick8(x, idx, run):
    r = np.arange(len(x))
    return x[r[:, None], idx[r % (8 * run) // run]]


E2M1 = np.array([0.0, 0.5, 1.0, 1.5, 2.0, 3.0, 4.0, 6.0, -0.0, -0.5, -1.0, -1.5, -2.0, -3.0, -4.0, -6.0])


def pack_weight(w, fmt):
    k, n = w.shape
    w = f64(np.asarray(w, np.float32).astype(ml_dtypes.bfloat16)).reshape(k // 32, 32, n)
    amax = np.abs(w).max(1)
    if fmt == "e4m3":
        byte = np.frexp(amax)[1] - 1 + 127 - 7
    else:
        mant, ex = np.frexp(amax / 6.0)
        byte = np.where(mant > 0.5, ex, ex - 1) + 127
    byte = np.clip(np.where(amax > 0, byte, 1), 1, 254)
    scaled = (w * np.exp2(127.0 - byte)[:, None, :]).reshape(k, n).astype(np.float32)
    by_word = np.ascontiguousarray(scaled.reshape(k // 512, 128, 4, n).transpose(0, 1, 3, 2))
    if fmt == "e4m3":
        words = by_word.astype(ml_dtypes.float8_e4m3fn).view(np.uint8)
    else:
        c = by_word.astype(ml_dtypes.float4_e2m1fn).view(np.uint8) & 0xF
        words = (c[..., 0::2] | (c[..., 1::2] << 4)).reshape(k // 512, 128, 2 * n)
    return np.ascontiguousarray(words), np.ascontiguousarray(byte.astype(np.uint8).reshape(k // 512, 16, n))


def unpack_weight(words, scales, fmt):
    g, _, n = scales.shape
    words = np.ascontiguousarray(words).reshape(g, 128, n, -1)
    if fmt == "e4m3":
        vals = words.view(ml_dtypes.float8_e4m3fn).astype(np.float64)
    else:
        nib = np.empty((g, 128, n, 4), np.uint8)
        nib[..., 0::2] = words & 0xF
        nib[..., 1::2] = words >> 4
        vals = E2M1[nib]
    vals = vals * np.repeat(np.exp2(scales.astype(np.float64) - 127.0), 8, axis=1)[..., None]
    return vals.transpose(0, 1, 3, 2).reshape(g * 512, n)


D, T, I, Q = 512, 1024, 512, 128


def setup_inputs():
    n = np.random.standard_normal
    idx = np.stack([np.random.permutation(T)[:I] for _ in range(8)])
    idx2 = np.stack([np.random.permutation(T)[:I] for _ in range(8)])
    idx3 = np.stack([np.random.permutation(T)[:I] for _ in range(8)])
    fd = mx_kscale(D)
    keysp = pack_weight(n((D, T)) / fd[:, None], "e2m1")
    return {
        "query": (n((D, Q)) * 0.9 / np.sqrt(D) * fd[:, None]).astype(np.float32),
        "query2": (n((D, Q)) * 0.9 / np.sqrt(D) * fd[:, None]).astype(np.float32),
        "keys_words": keysp[0],
        "keys_scales": keysp[1],
        "lam": (np.random.uniform(0.5, 1.5, (Q, 1))).astype(np.float32),
        "width": (np.random.uniform(0.3, 0.8, (Q, 1))).astype(np.float32),
        "old": (1.0 * n((Q, T))).astype(np.float32),
        "share2": (np.random.uniform(0.4, 1.2, (Q, 1))).astype(np.float32),
        "offs": striped8(idx),
        "offs2": striped8(idx2),
        "offs3": striped8(idx3),
    }


def reference(query, query2, keys_words, keys_scales, lam, width, old, share2, offs, offs2, offs3):
    idx = unstriped8(offs)
    idx2 = unstriped8(offs2)
    idx3 = unstriped8(offs3)
    keysu = unpack_weight(keys_words, keys_scales, "e2m1")
    queryq = mxq(f64(query), 0, "e4m3")
    a = queryq.T @ keysu
    query2q = mxq(f64(query2), 0, "e4m3")
    b = query2q.T @ keysu
    s = pick8(a, idx, 16) + pick8(a, idx2, 16) * np.tanh(pick8(b, idx, 16)) * f64(lam)
    ce = (s - np.mean(s, axis=1, keepdims=True)) / f64(width)
    p = 1.0 / (np.square(ce) + 1.0)
    w = p / np.sum(p, axis=1, keepdims=True)
    ws = w * 512.0
    f1 = np.zeros((Q, T))
    f1[np.arange(Q)[:, None], idx[np.arange(Q) % 128 // 16]] = ws
    f2 = np.zeros((Q, T))
    f2[np.arange(Q)[:, None], idx3[np.arange(Q) % 128 // 16]] = ws
    y = f64(old) + f1 + f2 * f64(share2)
    return y

@@ -1,0 +1,161 @@
+from contextlib import ExitStack
+
+import concourse.mybir as mybir
+
+D, T, I, Q = 512, 1024, 512, 128
+FLOPS = 2 * 2 * D * Q * T
+
+F32 = mybir.dt.float32
+BF16 = mybir.dt.bfloat16
+I32 = mybir.dt.int32
+U32 = mybir.dt.uint32
+U16 = mybir.dt.uint16
+U8 = mybir.dt.uint8
+FP8X4 = mybir.dt.float8_e4m3fn_x4
+FP4X4 = mybir.dt.float4_e2m1fn_x4
+ALU = mybir.AluOpType
+ACT = mybir.ActivationFunctionType
+
+P = 128
+PACK = 4
+N_MM = 256
+HALF = I // 2
+N_OUT = 256
+
+
+def tile_attend_turnedby_typical_twiceput_heads_kernel(
+    tc, query, query2, keys_words, keys_scales, lam, width, old, share2, offs, offs2, offs3, out
+):
+    nc = tc.nc
+    with ExitStack() as ctx:
+        sb = ctx.enter_context(tc.tile_pool(name="sb", bufs=1))
+        psum = ctx.enter_context(tc.psum_pool(name="psum", bufs=1))
+
+        list1 = sb.tile([P, I // 16], U16, name="list1")
+        list2 = sb.tile([P, I // 16], U16, name="list2")
+        list3 = sb.tile([P, I // 16], U16, name="list3")
+        key_words = sb.tile([P, 2 * T], U8, name="key_words", align_bytes=64)
+        key_scales = sb.tile([P, T], U8, name="key_scales", align_bytes=64)
+        raw_b = sb.tile([P, PACK, Q], F32, name="raw_b")
+        raw_a = sb.tile([P, PACK, Q], F32, name="raw_a")
+        lam_col = sb.tile([P, 1], F32, name="lam_col")
+        width_col = sb.tile([P, 1], F32, name="width_col")
+        share_col = sb.tile([P, 1], F32, name="share_col")
+        old_sb = sb.tile([P, T], F32, name="old_sb")
+        f1 = sb.tile([P, T], F32, name="f1")
+        f2 = sb.tile([P, T], F32, name="f2")
+
+        nc.vector.memset(key_scales[:].bitcast(I32), 0)
+        nc.sync.dma_start(raw_b[:], query2.rearrange("(p j) q -> p j q", j=PACK))
+        nc.sync.dma_start(raw_a[:], query.rearrange("(p j) q -> p j q", j=PACK))
+        nc.sync.dma_start(key_words[:], keys_words[0])
+        for quad in range(4):
+            nc.scalar.dma_start(
+                key_scales[32 * quad : 32 * quad + 4, :].bitcast(I32),
+                keys_scales[0, 4 * quad : 4 * quad + 4, :].bitcast(I32),
+            )
+        nc.sync.dma_start(list1[:], offs)
+        nc.sync.dma_start(list2[:], offs2)
+        nc.sync.dma_start(lam_col[:], lam)
+        nc.sync.dma_start(width_col[:], width)
+        nc.sync.dma_start(old_sb[:], old)
+        nc.sync.dma_start(list3[:], offs3)
+        nc.sync.dma_start(share_col[:], share2)
+        nc.vector.memset(f1[:], 0.0)
+        nc.vector.memset(f2[:], 0.0)
+
+        def quantise(raw, tag):
+            woven = sb.tile([P, Q, PACK], BF16, name="woven_" + tag, align_bytes=64)
+            codes = sb.tile([P, Q], U32, name="codes_" + tag, align_bytes=64)
+            scales = sb.tile([P, Q], U8, name="scales_" + tag, align_bytes=64)
+            nc.vector.tensor_copy(
+                woven[:].rearrange("p (c i) j -> p c j i", i=4),
+                raw[:].rearrange("p j (c i) -> p c j i", i=4),
+            )
+            nc.vector.quantize_mx(
+                out=codes[:].bitcast(FP8X4),
+                scales=scales[:],
+                in_=woven[:].rearrange("p q j -> p (q j)"),
+            )
+            return codes, scales
+
+        def score(codes, scales, tag):
+            scores = sb.tile([P, T], F32, name="scores_" + tag, tag="scores_" + tag)
+            for n0 in range(0, T, N_MM):
+                bank = psum.tile([P, N_MM], F32, name="bank_%s_%d" % (tag, n0))
+                nc.tensor.matmul_mx(
+                    out=bank[:],
+                    lhsT=codes[:].bitcast(FP8X4),
+                    lhsT_scale=scales[:],
+                    rhs=key_words[:, 2 * n0 : 2 * (n0 + N_MM)].bitcast(FP4X4),
+                    rhs_scale=key_scales[:, n0 : n0 + N_MM],
+                    start=True,
+                    stop=True,
+                )
+                nc.vector.tensor_copy(scores[:, n0 : n0 + N_MM], bank[:])
+            return scores
+
+        codes_b, scales_b = quantise(raw_b, "b")
+        codes_a, scales_a = quantise(raw_a, "a")
+        b = score(codes_b, scales_b, "b")
+        a = score(codes_a, scales_a, "a")
+
+        sig = sb.tile([P, I], F32, name="sig")
+        a1 = sb.tile([P, I], F32, name="a1")
+        a2 = sb.tile([P, I], F32, name="a2")
+        nc.scalar.activation(sig[:], b[:].indirect(list1[:]), ACT.Sigmoid, scale=2.0)
+        nc.scalar.activation(a1[:], a[:].indirect(list1[:]), ACT.Copy, scale=-1.0 / I)
+        for k in range(2):
+            nc.vector.tensor_copy(a2[:, HALF * k : HALF * (k + 1)], a[:].indirect(list2[:, 16 * k : 16 * (k + 1)]))
+        lam_scaled = sb.tile([P, 1], F32, name="lam_scaled")
+        nc.gpsimd.tensor_scalar(lam_scaled[:], lam_col[:], -2.0 / I, 0.0, ALU.mult, ALU.add)
+
+        width_sq = sb.tile([P, 1], F32, name="width_sq")
+        inv_width = sb.tile([P, 1], F32, name="inv_width", tag="scores_a")
+        inv_width_sq = sb.tile([P, 1], F32, name="inv_width_sq")
+        nc.gpsimd.tensor_tensor(width_sq[:], width_col[:], width_col[:], ALU.mult)
+        nc.scalar.activation(inv_width[:], width_sq[:], ACT.Abs_reciprocal_sqrt)
+
+        turned = sb.tile([P, I], F32, name="turned")
+        s_part = sb.tile([P, I], F32, name="s_part")
+        mean = sb.tile([P, 1], F32, name="mean")
+        halves = [slice(0, HALF), slice(HALF, I)]
+        for h in halves:
+            nc.vector.scalar_tensor_tensor(turned[:, h], sig[:, h], 0.5, a2[:, h], ALU.subtract, ALU.mult)
+        nc.vector.scalar_tensor_tensor(
+            s_part[:], turned[:], lam_scaled[:], a1[:], ALU.mult, ALU.add, accum_out=mean[:]
+        )
+
+        squared = sb.tile([P, I], F32, name="squared")
+        root = sb.tile([P, I], F32, name="root")
+        centred = sb.tile([P, HALF], F32, name="centred")
+        nc.scalar.activation(squared[:, :HALF], s_part[:, :HALF], ACT.Square, bias=mean[:], scale=-float(I))
+        nc.vector.tensor_scalar(centred[:], s_part[:, HALF:], -float(I), mean[:], ALU.mult, ALU.add)
+        nc.scalar.activation(inv_width_sq[:], inv_width[:], ACT.Square)
+        nc.vector.tensor_tensor(squared[:, HALF:], centred[:], centred[:], ALU.mult)
+        for h in halves:
+            nc.scalar.activation(root[:, h], squared[:, h], ACT.Abs_reciprocal_sqrt, bias=1.0, scale=inv_width_sq[:])
+
+        part = sb.tile([P, I], F32, name="part")
+        part_sum = sb.tile([P, 1], F32, name="part_sum")
+        inv_sum = sb.tile([P, 1], F32, name="inv_sum")
+        ws = sb.tile([P, I], F32, name="ws")
+        nc.vector.scalar_tensor_tensor(
+            part[:], root[:], 1.0, root[:], ALU.mult, ALU.mult, accum_out=part_sum[:]
+        )
+        nc.vector.reciprocal(inv_sum[:], part_sum[:])
+        nc.vector.tensor_scalar(ws[:], part[:], inv_sum[:], 512.0, ALU.mult, ALU.mult)
+
+        nc.vector.tensor_copy(f1[:].indirect(list1[:]), ws[:])
+        nc.vector.tensor_copy(f2[:].indirect(list3[:]), ws[:])
+
+        base = sb.tile([P, T], F32, name="base")
+        nc.gpsimd.tensor_tensor(base[:], old_sb[:], f1[:], ALU.add)
+        result = sb.tile([P, T], F32, name="result")
+        queues = [nc.sync, nc.scalar]
+        for k, n0 in enumerate(range(0, T, N_OUT)):
+            cols = slice(n0, n0 + N_OUT)
+            nc.vector.scalar_tensor_tensor(
+                result[:, cols], f2[:, cols], share_col[:], base[:, cols], ALU.mult, ALU.add
+            )
+            queues[k % 2].dma_start(out[:, cols], result[:, cols])

@@ -1,6 +1,7 @@
 from contextlib import ExitStack
 
 import concourse.mybir as mybir
+from concourse.masks import make_identity
 
 D, T, I, Q = 512, 1024, 512, 128
 FLOPS = 2 * 2 * D * Q * T
@@ -20,7 +21,7 @@ P = 128
 PACK = 4
 N_MM = 256
 HALF = I // 2
-N_OUT = 256
+FIRST = 128
 
 
 def tile_attend_turnedby_typical_twiceput_heads_kernel(
@@ -47,8 +48,8 @@ def tile_attend_turnedby_typical_twiceput_heads_kernel(
 
         nc.vector.memset(key_scales[:].bitcast(I32), 0)
         nc.sync.dma_start(raw_b[:], query2.rearrange("(p j) q -> p j q", j=PACK))
-        nc.sync.dma_start(raw_a[:], query.rearrange("(p j) q -> p j q", j=PACK))
         nc.sync.dma_start(key_words[:], keys_words[0])
+        nc.sync.dma_start(raw_a[:], query.rearrange("(p j) q -> p j q", j=PACK))
         for quad in range(4):
             nc.scalar.dma_start(
                 key_scales[32 * quad : 32 * quad + 4, :].bitcast(I32),
@@ -63,10 +64,12 @@ def tile_attend_turnedby_typical_twiceput_heads_kernel(
         nc.sync.dma_start(share_col[:], share2)
         nc.vector.memset(f1[:], 0.0)
         nc.vector.memset(f2[:], 0.0)
+        ident = sb.tile([P, P], F32, name="ident")
+        make_identity(nc, ident[:])
 
         def quantise(raw, tag):
             woven = sb.tile([P, Q, PACK], BF16, name="woven_" + tag, align_bytes=64)
-            codes = sb.tile([P, Q], U32, name="codes_" + tag, align_bytes=64)
+            codes = sb.tile([P, Q], U32, name="codes_" + tag, tag="codes_" + tag, align_bytes=64)
             scales = sb.tile([P, Q], U8, name="scales_" + tag, align_bytes=64)
             nc.vector.tensor_copy(
                 woven[:].rearrange("p (c i) j -> p c j i", i=4),
@@ -82,7 +85,7 @@ def tile_attend_turnedby_typical_twiceput_heads_kernel(
         def score(codes, scales, tag):
             scores = sb.tile([P, T], F32, name="scores_" + tag, tag="scores_" + tag)
             for n0 in range(0, T, N_MM):
-                bank = psum.tile([P, N_MM], F32, name="bank_%s_%d" % (tag, n0))
+                bank = psum.tile([P, N_MM], F32, name="bank_%s_%d" % (tag, n0), tag="bank_%s_%d" % (tag, n0))
                 nc.tensor.matmul_mx(
                     out=bank[:],
                     lhsT=codes[:].bitcast(FP8X4),
@@ -104,16 +107,14 @@ def tile_attend_turnedby_typical_twiceput_heads_kernel(
         a1 = sb.tile([P, I], F32, name="a1")
         a2 = sb.tile([P, I], F32, name="a2")
         nc.scalar.activation(sig[:], b[:].indirect(list1[:]), ACT.Sigmoid, scale=2.0)
-        nc.scalar.activation(a1[:], a[:].indirect(list1[:]), ACT.Copy, scale=-1.0 / I)
+        nc.scalar.activation(a1[:], a[:].indirect(list1[:]), ACT.Copy, scale=0.5)
         for k in range(2):
             nc.vector.tensor_copy(a2[:, HALF * k : HALF * (k + 1)], a[:].indirect(list2[:, 16 * k : 16 * (k + 1)]))
-        lam_scaled = sb.tile([P, 1], F32, name="lam_scaled")
-        nc.gpsimd.tensor_scalar(lam_scaled[:], lam_col[:], -2.0 / I, 0.0, ALU.mult, ALU.add)
 
-        width_sq = sb.tile([P, 1], F32, name="width_sq")
-        inv_width = sb.tile([P, 1], F32, name="inv_width", tag="scores_a")
+        width_sq = sb.tile([P, 1], F32, name="width_sq", tag="codes_a", align_bytes=64)
+        inv_width = sb.tile([P, 1], F32, name="inv_width")
         inv_width_sq = sb.tile([P, 1], F32, name="inv_width_sq")
-        nc.gpsimd.tensor_tensor(width_sq[:], width_col[:], width_col[:], ALU.mult)
+        nc.vector.tensor_tensor(width_sq[:], width_col[:], width_col[:], ALU.mult)
         nc.scalar.activation(inv_width[:], width_sq[:], ACT.Abs_reciprocal_sqrt)
 
         turned = sb.tile([P, I], F32, name="turned")
@@ -123,16 +124,14 @@ def tile_attend_turnedby_typical_twiceput_heads_kernel(
         for h in halves:
             nc.vector.scalar_tensor_tensor(turned[:, h], sig[:, h], 0.5, a2[:, h], ALU.subtract, ALU.mult)
         nc.vector.scalar_tensor_tensor(
-            s_part[:], turned[:], lam_scaled[:], a1[:], ALU.mult, ALU.add, accum_out=mean[:]
+            s_part[:], turned[:], lam_col[:], a1[:], ALU.mult, ALU.add, accum_out=mean[:]
         )
 
         squared = sb.tile([P, I], F32, name="squared")
         root = sb.tile([P, I], F32, name="root")
-        centred = sb.tile([P, HALF], F32, name="centred")
         nc.scalar.activation(squared[:, :HALF], s_part[:, :HALF], ACT.Square, bias=mean[:], scale=-float(I))
-        nc.vector.tensor_scalar(centred[:], s_part[:, HALF:], -float(I), mean[:], ALU.mult, ALU.add)
-        nc.scalar.activation(inv_width_sq[:], inv_width[:], ACT.Square)
-        nc.vector.tensor_tensor(squared[:, HALF:], centred[:], centred[:], ALU.mult)
+        nc.scalar.activation(inv_width_sq[:], inv_width[:], ACT.Square, scale=2.0 / I)
+        nc.scalar.activation(squared[:, HALF:], s_part[:, HALF:], ACT.Square, bias=mean[:], scale=-float(I))
         for h in halves:
             nc.scalar.activation(root[:, h], squared[:, h], ACT.Abs_reciprocal_sqrt, bias=1.0, scale=inv_width_sq[:])
 
@@ -144,18 +143,42 @@ def tile_attend_turnedby_typical_twiceput_heads_kernel(
             part[:], root[:], 1.0, root[:], ALU.mult, ALU.mult, accum_out=part_sum[:]
         )
         nc.vector.reciprocal(inv_sum[:], part_sum[:])
-        nc.vector.tensor_scalar(ws[:], part[:], inv_sum[:], 512.0, ALU.mult, ALU.mult)
+        for cols in (slice(0, FIRST), slice(FIRST, I)):
+            nc.vector.tensor_scalar(ws[:, cols], part[:, cols], inv_sum[:], 512.0, ALU.mult, ALU.mult)
 
+        nc.vector.tensor_copy(f2[:].indirect(list3[:, : FIRST // 16]), ws[:, :FIRST])
         nc.vector.tensor_copy(f1[:].indirect(list1[:]), ws[:])
-        nc.vector.tensor_copy(f2[:].indirect(list3[:]), ws[:])
+        nc.vector.tensor_copy(f2[:].indirect(list3[:, FIRST // 16 :]), ws[:, FIRST:])
 
-        base = sb.tile([P, T], F32, name="base")
-        nc.gpsimd.tensor_tensor(base[:], old_sb[:], f1[:], ALU.add)
+        blocks = N_MM // P
+        turned_banks = []
+        for n0 in range(0, T, N_MM):
+            bank = psum.tile([P, N_MM], F32, name="sum_turned_%d" % n0, tag="bank_b_%d" % n0)
+            turned_banks.append(bank)
+            for j in range(blocks):
+                nc.tensor.matmul(
+                    bank[:, j * P : (j + 1) * P], old_sb[:, n0 + j * P : n0 + (j + 1) * P], ident[:],
+                    start=(j == 0), stop=False, is_transpose=True,
+                )
+        base_turned = sb.tile([P, T], F32, name="base_turned")
+        for k, n0 in enumerate(range(0, T, N_MM)):
+            bank = turned_banks[k]
+            for j in range(blocks):
+                nc.tensor.matmul(
+                    bank[:, j * P : (j + 1) * P], f1[:, n0 + j * P : n0 + (j + 1) * P], ident[:],
+                    start=False, stop=(j == blocks - 1), is_transpose=True,
+                )
+            nc.scalar.copy(base_turned[:, n0 : n0 + N_MM], bank[:])
         result = sb.tile([P, T], F32, name="result")
         queues = [nc.sync, nc.scalar]
-        for k, n0 in enumerate(range(0, T, N_OUT)):
-            cols = slice(n0, n0 + N_OUT)
+        for k, n0 in enumerate(range(0, T, N_MM)):
+            base = psum.tile([P, N_MM], F32, name="base_%d" % n0, tag="bank_a_%d" % n0)
+            for j in range(blocks):
+                nc.tensor.transpose(
+                    base[:, j * P : (j + 1) * P], base_turned[:, n0 + j * P : n0 + (j + 1) * P], ident[:]
+                )
+            cols = slice(n0, n0 + N_MM)
             nc.vector.scalar_tensor_tensor(
-                result[:, cols], f2[:, cols], share_col[:], base[:, cols], ALU.mult, ALU.add
+                result[:, cols], f2[:, cols], share_col[:], base[:], ALU.mult, ALU.add
             )
             queues[k % 2].dma_start(out[:, cols], result[:, cols])

@@ -22,6 +22,8 @@ PACK = 4
 N_MM = 256
 HALF = I // 2
 FIRST = 128
+PIECES = (256, 256, 256, 128, 128)
+T_PE = 512
 
 
 def tile_attend_turnedby_typical_twiceput_heads_kernel(
@@ -35,31 +37,38 @@ def tile_attend_turnedby_typical_twiceput_heads_kernel(
         list1 = sb.tile([P, I // 16], U16, name="list1")
         list2 = sb.tile([P, I // 16], U16, name="list2")
         list3 = sb.tile([P, I // 16], U16, name="list3")
-        key_words = sb.tile([P, 2 * T], U8, name="key_words", align_bytes=64)
+        key_words = [sb.tile([P, T], U8, name="key_words_%d" % h, align_bytes=64) for h in range(2)]
         key_scales = sb.tile([P, T], U8, name="key_scales", align_bytes=64)
         raw_b = sb.tile([P, PACK, Q], F32, name="raw_b")
         raw_a = sb.tile([P, PACK, Q], F32, name="raw_a")
         lam_col = sb.tile([P, 1], F32, name="lam_col")
         width_col = sb.tile([P, 1], F32, name="width_col")
         share_col = sb.tile([P, 1], F32, name="share_col")
-        old_sb = sb.tile([P, T], F32, name="old_sb")
+        old_first = sb.tile([P, N_MM], F32, name="old_first", tag="old_first")
+        old_rest = sb.tile([P, T - N_MM], F32, name="old_rest")
         f1 = sb.tile([P, T], F32, name="f1")
         f2 = sb.tile([P, T], F32, name="f2")
 
         nc.vector.memset(key_scales[:].bitcast(I32), 0)
+        warm_in = sb.tile([P, 1], F32, name="warm_in")
+        warm_out = sb.tile([P, 1], F32, name="warm_out")
+        nc.vector.memset(warm_in[:], 0.0)
+        nc.scalar.activation(warm_out[:], warm_in[:], ACT.Sigmoid)
         nc.sync.dma_start(raw_b[:], query2.rearrange("(p j) q -> p j q", j=PACK))
-        nc.sync.dma_start(key_words[:], keys_words[0])
-        nc.sync.dma_start(raw_a[:], query.rearrange("(p j) q -> p j q", j=PACK))
+        nc.sync.dma_start(key_words[0][:], keys_words[0, :, :T])
         for quad in range(4):
-            nc.scalar.dma_start(
+            nc.sync.dma_start(
                 key_scales[32 * quad : 32 * quad + 4, :].bitcast(I32),
                 keys_scales[0, 4 * quad : 4 * quad + 4, :].bitcast(I32),
             )
+        nc.sync.dma_start(raw_a[:], query.rearrange("(p j) q -> p j q", j=PACK))
+        nc.sync.dma_start(key_words[1][:], keys_words[0, :, T:])
         nc.sync.dma_start(list1[:], offs)
         nc.sync.dma_start(list2[:], offs2)
-        nc.sync.dma_start(lam_col[:], lam)
+        nc.sync.dma_start(old_first[:], old[:, :N_MM])
         nc.sync.dma_start(width_col[:], width)
-        nc.sync.dma_start(old_sb[:], old)
+        nc.sync.dma_start(lam_col[:], lam)
+        nc.sync.dma_start(old_rest[:], old[:, N_MM:])
         nc.sync.dma_start(list3[:], offs3)
         nc.sync.dma_start(share_col[:], share2)
         nc.vector.memset(f1[:], 0.0)
@@ -69,7 +78,7 @@ def tile_attend_turnedby_typical_twiceput_heads_kernel(
 
         def quantise(raw, tag):
             woven = sb.tile([P, Q, PACK], BF16, name="woven_" + tag, align_bytes=64)
-            codes = sb.tile([P, Q], U32, name="codes_" + tag, tag="codes_" + tag, align_bytes=64)
+            codes = sb.tile([P, Q], U32, name="codes_" + tag, align_bytes=64)
             scales = sb.tile([P, Q], U8, name="scales_" + tag, align_bytes=64)
             nc.vector.tensor_copy(
                 woven[:].rearrange("p (c i) j -> p c j i", i=4),
@@ -82,26 +91,40 @@ def tile_attend_turnedby_typical_twiceput_heads_kernel(
             )
             return codes, scales
 
-        def score(codes, scales, tag):
-            scores = sb.tile([P, T], F32, name="scores_" + tag, tag="scores_" + tag)
-            for n0 in range(0, T, N_MM):
-                bank = psum.tile([P, N_MM], F32, name="bank_%s_%d" % (tag, n0), tag="bank_%s_%d" % (tag, n0))
+        def score(codes, scales, tag, empty_bank, first_bank):
+            scores = sb.tile([P, T], F32, name="scores_" + tag)
+            n0 = 0
+            for k, n in enumerate(PIECES):
+                bank = psum.tile([P, n], F32, name="bank_%s_%d" % (tag, k), tag="bank%d" % ((first_bank + k) % 8))
+                words, w0 = key_words[n0 // (T // 2)], 2 * (n0 % (T // 2))
                 nc.tensor.matmul_mx(
                     out=bank[:],
                     lhsT=codes[:].bitcast(FP8X4),
                     lhsT_scale=scales[:],
-                    rhs=key_words[:, 2 * n0 : 2 * (n0 + N_MM)].bitcast(FP4X4),
-                    rhs_scale=key_scales[:, n0 : n0 + N_MM],
+                    rhs=words[:, w0 : w0 + 2 * n].bitcast(FP4X4),
+                    rhs_scale=key_scales[:, n0 : n0 + n],
                     start=True,
                     stop=True,
                 )
-                nc.vector.tensor_copy(scores[:, n0 : n0 + N_MM], bank[:])
+                empty_bank(scores[:, n0 : n0 + n], bank[:])
+                n0 = n0 + n
             return scores
 
         codes_b, scales_b = quantise(raw_b, "b")
         codes_a, scales_a = quantise(raw_a, "a")
-        b = score(codes_b, scales_b, "b")
-        a = score(codes_a, scales_a, "a")
+        b = score(codes_b, scales_b, "b", nc.scalar.copy, 0)
+        a = score(codes_a, scales_a, "a", nc.vector.tensor_copy, len(PIECES))
+
+        blocks = N_MM // P
+        turned_banks = []
+        for n0, old_part in ((0, old_first), (N_MM, old_rest)):
+            bank = psum.tile([P, N_MM], F32, name="sum_turned_%d" % n0, tag="bank%d" % (1 - n0 // N_MM))
+            turned_banks.append(bank)
+            for j in range(blocks):
+                nc.tensor.matmul(
+                    bank[:, j * P : (j + 1) * P], old_part[:, j * P : (j + 1) * P], ident[:],
+                    start=(j == 0), stop=False, is_transpose=True,
+                )
 
         sig = sb.tile([P, I], F32, name="sig")
         a1 = sb.tile([P, I], F32, name="a1")
@@ -111,11 +134,9 @@ def tile_attend_turnedby_typical_twiceput_heads_kernel(
         for k in range(2):
             nc.vector.tensor_copy(a2[:, HALF * k : HALF * (k + 1)], a[:].indirect(list2[:, 16 * k : 16 * (k + 1)]))
 
-        width_sq = sb.tile([P, 1], F32, name="width_sq", tag="codes_a", align_bytes=64)
-        inv_width = sb.tile([P, 1], F32, name="inv_width")
+        inv_width = sb.tile([P, 1], F32, name="inv_width", tag="old_first")
         inv_width_sq = sb.tile([P, 1], F32, name="inv_width_sq")
-        nc.vector.tensor_tensor(width_sq[:], width_col[:], width_col[:], ALU.mult)
-        nc.scalar.activation(inv_width[:], width_sq[:], ACT.Abs_reciprocal_sqrt)
+        nc.scalar.activation(inv_width[:], width_col[:], ACT.Abs_reciprocal_sqrt, scale=width_col[:])
 
         turned = sb.tile([P, I], F32, name="turned")
         s_part = sb.tile([P, I], F32, name="s_part")
@@ -150,18 +171,8 @@ def tile_attend_turnedby_typical_twiceput_heads_kernel(
         nc.vector.tensor_copy(f1[:].indirect(list1[:]), ws[:])
         nc.vector.tensor_copy(f2[:].indirect(list3[:, FIRST // 16 :]), ws[:, FIRST:])
 
-        blocks = N_MM // P
-        turned_banks = []
-        for n0 in range(0, T, N_MM):
-            bank = psum.tile([P, N_MM], F32, name="sum_turned_%d" % n0, tag="bank_b_%d" % n0)
-            turned_banks.append(bank)
-            for j in range(blocks):
-                nc.tensor.matmul(
-                    bank[:, j * P : (j + 1) * P], old_sb[:, n0 + j * P : n0 + (j + 1) * P], ident[:],
-                    start=(j == 0), stop=False, is_transpose=True,
-                )
-        base_turned = sb.tile([P, T], F32, name="base_turned")
-        for k, n0 in enumerate(range(0, T, N_MM)):
+        base_turned = sb.tile([P, T_PE], F32, name="base_turned")
+        for k, n0 in enumerate(range(0, T_PE, N_MM)):
             bank = turned_banks[k]
             for j in range(blocks):
                 nc.tensor.matmul(
@@ -169,16 +180,21 @@ def tile_attend_turnedby_typical_twiceput_heads_kernel(
                     start=False, stop=(j == blocks - 1), is_transpose=True,
                 )
             nc.scalar.copy(base_turned[:, n0 : n0 + N_MM], bank[:])
+        base_rest = sb.tile([P, T - T_PE], F32, name="base_rest")
+        nc.gpsimd.tensor_tensor(base_rest[:], old_rest[:, T_PE - N_MM :], f1[:, T_PE:], ALU.add)
+
         result = sb.tile([P, T], F32, name="result")
         queues = [nc.sync, nc.scalar]
         for k, n0 in enumerate(range(0, T, N_MM)):
-            base = psum.tile([P, N_MM], F32, name="base_%d" % n0, tag="bank_a_%d" % n0)
-            for j in range(blocks):
-                nc.tensor.transpose(
-                    base[:, j * P : (j + 1) * P], base_turned[:, n0 + j * P : n0 + (j + 1) * P], ident[:]
-                )
             cols = slice(n0, n0 + N_MM)
-            nc.vector.scalar_tensor_tensor(
-                result[:, cols], f2[:, cols], share_col[:], base[:], ALU.mult, ALU.add
-            )
+            if n0 < T_PE:
+                bank = psum.tile([P, N_MM], F32, name="base_%d" % n0, tag="bank%d" % (2 + k))
+                for j in range(blocks):
+                    nc.tensor.transpose(
+                        bank[:, j * P : (j + 1) * P], base_turned[:, n0 + j * P : n0 + (j + 1) * P], ident[:]
+                    )
+                base = bank[:]
+            else:
+                base = base_rest[:, n0 - T_PE : n0 - T_PE + N_MM]
+            nc.vector.scalar_tensor_tensor(result[:, cols], f2[:, cols], share_col[:], base, ALU.mult, ALU.add)
             queues[k % 2].dma_start(out[:, cols], result[:, cols])

@@ -22,6 +22,8 @@ PACK = 4
 N_MM = 256
 HALF = I // 2
 FIRST = 128
+LEAD = 352
+CAST_SPLIT = 80
 PIECES = (256, 256, 256, 128, 128)
 T_PE = 512
 
@@ -76,14 +78,15 @@ def tile_attend_turnedby_typical_twiceput_heads_kernel(
         ident = sb.tile([P, P], F32, name="ident")
         make_identity(nc, ident[:])
 
-        def quantise(raw, tag):
+        def quantise(raw, tag, shares):
             woven = sb.tile([P, Q, PACK], BF16, name="woven_" + tag, align_bytes=64)
             codes = sb.tile([P, Q], U32, name="codes_" + tag, align_bytes=64)
             scales = sb.tile([P, Q], U8, name="scales_" + tag, align_bytes=64)
-            nc.vector.tensor_copy(
-                woven[:].rearrange("p (c i) j -> p c j i", i=4),
-                raw[:].rearrange("p j (c i) -> p c j i", i=4),
-            )
+            for cast, cols in shares:
+                cast(
+                    woven[:, cols, :].rearrange("p (c i) j -> p c j i", i=4),
+                    raw[:, :, cols].rearrange("p j (c i) -> p c j i", i=4),
+                )
             nc.vector.quantize_mx(
                 out=codes[:].bitcast(FP8X4),
                 scales=scales[:],
@@ -110,8 +113,10 @@ def tile_attend_turnedby_typical_twiceput_heads_kernel(
                 n0 = n0 + n
             return scores
 
-        codes_b, scales_b = quantise(raw_b, "b")
-        codes_a, scales_a = quantise(raw_a, "a")
+        codes_b, scales_b = quantise(
+            raw_b, "b", [(nc.vector.tensor_copy, slice(0, CAST_SPLIT)), (nc.scalar.copy, slice(CAST_SPLIT, Q))]
+        )
+        codes_a, scales_a = quantise(raw_a, "a", [(nc.vector.tensor_copy, slice(0, Q))])
         b = score(codes_b, scales_b, "b", nc.scalar.copy, 0)
         a = score(codes_a, scales_a, "a", nc.vector.tensor_copy, len(PIECES))
 
@@ -150,22 +155,32 @@ def tile_attend_turnedby_typical_twiceput_heads_kernel(
 
         squared = sb.tile([P, I], F32, name="squared")
         root = sb.tile([P, I], F32, name="root")
-        nc.scalar.activation(squared[:, :HALF], s_part[:, :HALF], ACT.Square, bias=mean[:], scale=-float(I))
+        lead, rest = slice(0, LEAD), slice(LEAD, I)
+        nc.scalar.activation(squared[:, lead], s_part[:, lead], ACT.Square, bias=mean[:], scale=-float(I))
         nc.scalar.activation(inv_width_sq[:], inv_width[:], ACT.Square, scale=2.0 / I)
-        nc.scalar.activation(squared[:, HALF:], s_part[:, HALF:], ACT.Square, bias=mean[:], scale=-float(I))
-        for h in halves:
-            nc.scalar.activation(root[:, h], squared[:, h], ACT.Abs_reciprocal_sqrt, bias=1.0, scale=inv_width_sq[:])
+        nc.scalar.activation(squared[:, rest], s_part[:, rest], ACT.Square, bias=mean[:], scale=-float(I))
+        for cols in (lead, rest):
+            nc.scalar.activation(
+                root[:, cols], squared[:, cols], ACT.Abs_reciprocal_sqrt, bias=1.0, scale=inv_width_sq[:]
+            )
 
         part = sb.tile([P, I], F32, name="part")
-        part_sum = sb.tile([P, 1], F32, name="part_sum")
-        inv_sum = sb.tile([P, 1], F32, name="inv_sum")
+        sum_lead = sb.tile([P, 1], F32, name="sum_lead")
+        sum_rest = sb.tile([P, 1], F32, name="sum_rest")
+        norm_root = sb.tile([P, 1], F32, name="norm_root")
+        norm_rest = sb.tile([P, 1], F32, name="norm_rest")
         ws = sb.tile([P, I], F32, name="ws")
         nc.vector.scalar_tensor_tensor(
-            part[:], root[:], 1.0, root[:], ALU.mult, ALU.mult, accum_out=part_sum[:]
+            part[:, lead], root[:, lead], 1.0, root[:, lead], ALU.mult, ALU.mult, accum_out=sum_lead[:]
         )
-        nc.vector.reciprocal(inv_sum[:], part_sum[:])
-        for cols in (slice(0, FIRST), slice(FIRST, I)):
-            nc.vector.tensor_scalar(ws[:, cols], part[:, cols], inv_sum[:], 512.0, ALU.mult, ALU.mult)
+        nc.scalar.activation(part[:, rest], root[:, rest], ACT.Square, scale=512.0**-0.5, accum_out=sum_rest[:])
+        nc.scalar.activation(
+            norm_root[:], sum_lead[:], ACT.Abs_reciprocal_sqrt, bias=sum_rest[:], scale=1.0 / 512.0
+        )
+        for cols in (slice(0, FIRST), slice(FIRST, LEAD)):
+            nc.vector.tensor_scalar(ws[:, cols], part[:, cols], norm_root[:], norm_root[:], ALU.mult, ALU.mult)
+        nc.vector.tensor_scalar(norm_rest[:], norm_root[:], norm_root[:], 512.0, ALU.mult, ALU.mult)
+        nc.scalar.activation(ws[:, rest], part[:, rest], ACT.Copy, scale=norm_rest[:])
 
         nc.vector.tensor_copy(f2[:].indirect(list3[:, : FIRST // 16]), ws[:, :FIRST])
         nc.vector.tensor_copy(f1[:].indirect(list1[:]), ws[:])

from contextlib import ExitStack

import concourse.mybir as mybir
from concourse.masks import make_identity

D, T, I, Q = 512, 1024, 512, 128
FLOPS = 2 * 2 * D * Q * T

F32 = mybir.dt.float32
BF16 = mybir.dt.bfloat16
I32 = mybir.dt.int32
U32 = mybir.dt.uint32
U16 = mybir.dt.uint16
U8 = mybir.dt.uint8
FP8X4 = mybir.dt.float8_e4m3fn_x4
FP4X4 = mybir.dt.float4_e2m1fn_x4
ALU = mybir.AluOpType
ACT = mybir.ActivationFunctionType

P = 128
PACK = 4
N_MM = 256
HALF = I // 2
FIRST = 128
LEAD = 352
CAST_SPLIT = 80
PIECES = (256, 256, 256, 128, 128)
T_PE = 512


def tile_attend_turnedby_typical_twiceput_heads_kernel(
    tc, query, query2, keys_words, keys_scales, lam, width, old, share2, offs, offs2, offs3, out
):
    nc = tc.nc
    with ExitStack() as ctx:
        sb = ctx.enter_context(tc.tile_pool(name="sb", bufs=1))
        psum = ctx.enter_context(tc.psum_pool(name="psum", bufs=1))

        list1 = sb.tile([P, I // 16], U16, name="list1")
        list2 = sb.tile([P, I // 16], U16, name="list2")
        list3 = sb.tile([P, I // 16], U16, name="list3")
        key_words = [sb.tile([P, T], U8, name="key_words_%d" % h, align_bytes=64) for h in range(2)]
        key_scales = sb.tile([P, T], U8, name="key_scales", align_bytes=64)
        raw_b = sb.tile([P, PACK, Q], F32, name="raw_b")
        raw_a = sb.tile([P, PACK, Q], F32, name="raw_a")
        lam_col = sb.tile([P, 1], F32, name="lam_col")
        width_col = sb.tile([P, 1], F32, name="width_col")
        share_col = sb.tile([P, 1], F32, name="share_col")
        old_first = sb.tile([P, N_MM], F32, name="old_first", tag="old_first")
        old_rest = sb.tile([P, T - N_MM], F32, name="old_rest")
        f1 = sb.tile([P, T], F32, name="f1")
        f2 = sb.tile([P, T], F32, name="f2")

        nc.vector.memset(key_scales[:].bitcast(I32), 0)
        warm_in = sb.tile([P, 1], F32, name="warm_in")
        warm_out = sb.tile([P, 1], F32, name="warm_out")
        nc.vector.memset(warm_in[:], 0.0)
        nc.scalar.activation(warm_out[:], warm_in[:], ACT.Sigmoid)
        nc.sync.dma_start(raw_b[:], query2.rearrange("(p j) q -> p j q", j=PACK))
        nc.sync.dma_start(key_words[0][:], keys_words[0, :, :T])
        for quad in range(4):
            nc.sync.dma_start(
                key_scales[32 * quad : 32 * quad + 4, :].bitcast(I32),
                keys_scales[0, 4 * quad : 4 * quad + 4, :].bitcast(I32),
            )
        nc.sync.dma_start(raw_a[:], query.rearrange("(p j) q -> p j q", j=PACK))
        nc.sync.dma_start(key_words[1][:], keys_words[0, :, T:])
        nc.sync.dma_start(list1[:], offs)
        nc.sync.dma_start(list2[:], offs2)
        nc.sync.dma_start(old_first[:], old[:, :N_MM])
        nc.sync.dma_start(width_col[:], width)
        nc.sync.dma_start(lam_col[:], lam)
        nc.sync.dma_start(old_rest[:], old[:, N_MM:])
        nc.sync.dma_start(list3[:], offs3)
        nc.sync.dma_start(share_col[:], share2)
        nc.vector.memset(f1[:], 0.0)
        nc.vector.memset(f2[:], 0.0)
        ident = sb.tile([P, P], F32, name="ident")
        make_identity(nc, ident[:])

        def quantise(raw, tag, shares):
            woven = sb.tile([P, Q, PACK], BF16, name="woven_" + tag, align_bytes=64)
            codes = sb.tile([P, Q], U32, name="codes_" + tag, align_bytes=64)
            scales = sb.tile([P, Q], U8, name="scales_" + tag, align_bytes=64)
            for cast, cols in shares:
                cast(
                    woven[:, cols, :].rearrange("p (c i) j -> p c j i", i=4),
                    raw[:, :, cols].rearrange("p j (c i) -> p c j i", i=4),
                )
            nc.vector.quantize_mx(
                out=codes[:].bitcast(FP8X4),
                scales=scales[:],
                in_=woven[:].rearrange("p q j -> p (q j)"),
            )
            return codes, scales

        def score(codes, scales, tag, empty_bank, first_bank):
            scores = sb.tile([P, T], F32, name="scores_" + tag)
            n0 = 0
            for k, n in enumerate(PIECES):
                bank = psum.tile([P, n], F32, name="bank_%s_%d" % (tag, k), tag="bank%d" % ((first_bank + k) % 8))
                words, w0 = key_words[n0 // (T // 2)], 2 * (n0 % (T // 2))
                nc.tensor.matmul_mx(
                    out=bank[:],
                    lhsT=codes[:].bitcast(FP8X4),
                    lhsT_scale=scales[:],
                    rhs=words[:, w0 : w0 + 2 * n].bitcast(FP4X4),
                    rhs_scale=key_scales[:, n0 : n0 + n],
                    start=True,
                    stop=True,
                )
                empty_bank(scores[:, n0 : n0 + n], bank[:])
                n0 = n0 + n
            return scores

        codes_b, scales_b = quantise(
            raw_b, "b", [(nc.vector.tensor_copy, slice(0, CAST_SPLIT)), (nc.scalar.copy, slice(CAST_SPLIT, Q))]
        )
        codes_a, scales_a = quantise(raw_a, "a", [(nc.vector.tensor_copy, slice(0, Q))])
        b = score(codes_b, scales_b, "b", nc.scalar.copy, 0)
        a = score(codes_a, scales_a, "a", nc.vector.tensor_copy, len(PIECES))

        blocks = N_MM // P
        turned_banks = []
        for n0, old_part in ((0, old_first), (N_MM, old_rest)):
            bank = psum.tile([P, N_MM], F32, name="sum_turned_%d" % n0, tag="bank%d" % (1 - n0 // N_MM))
            turned_banks.append(bank)
            for j in range(blocks):
                nc.tensor.matmul(
                    bank[:, j * P : (j + 1) * P], old_part[:, j * P : (j + 1) * P], ident[:],
                    start=(j == 0), stop=False, is_transpose=True,
                )

        sig = sb.tile([P, I], F32, name="sig")
        a1 = sb.tile([P, I], F32, name="a1")
        a2 = sb.tile([P, I], F32, name="a2")
        nc.scalar.activation(sig[:], b[:].indirect(list1[:]), ACT.Sigmoid, scale=2.0)
        nc.scalar.activation(a1[:], a[:].indirect(list1[:]), ACT.Copy, scale=0.5)
        for k in range(2):
            nc.vector.tensor_copy(a2[:, HALF * k : HALF * (k + 1)], a[:].indirect(list2[:, 16 * k : 16 * (k + 1)]))

        inv_width = sb.tile([P, 1], F32, name="inv_width", tag="old_first")
        inv_width_sq = sb.tile([P, 1], F32, name="inv_width_sq")
        nc.scalar.activation(inv_width[:], width_col[:], ACT.Abs_reciprocal_sqrt, scale=width_col[:])

        turned = sb.tile([P, I], F32, name="turned")
        s_part = sb.tile([P, I], F32, name="s_part")
        mean = sb.tile([P, 1], F32, name="mean")
        halves = [slice(0, HALF), slice(HALF, I)]
        for h in halves:
            nc.vector.scalar_tensor_tensor(turned[:, h], sig[:, h], 0.5, a2[:, h], ALU.subtract, ALU.mult)
        nc.vector.scalar_tensor_tensor(
            s_part[:], turned[:], lam_col[:], a1[:], ALU.mult, ALU.add, accum_out=mean[:]
        )

        squared = sb.tile([P, I], F32, name="squared")
        root = sb.tile([P, I], F32, name="root")
        lead, rest = slice(0, LEAD), slice(LEAD, I)
        nc.scalar.activation(squared[:, lead], s_part[:, lead], ACT.Square, bias=mean[:], scale=-float(I))
        nc.scalar.activation(inv_width_sq[:], inv_width[:], ACT.Square, scale=2.0 / I)
        nc.scalar.activation(squared[:, rest], s_part[:, rest], ACT.Square, bias=mean[:], scale=-float(I))
        for cols in (lead, rest):
            nc.scalar.activation(
                root[:, cols], squared[:, cols], ACT.Abs_reciprocal_sqrt, bias=1.0, scale=inv_width_sq[:]
            )

        part = sb.tile([P, I], F32, name="part")
        sum_lead = sb.tile([P, 1], F32, name="sum_lead")
        sum_rest = sb.tile([P, 1], F32, name="sum_rest")
        norm_root = sb.tile([P, 1], F32, name="norm_root")
        norm_rest = sb.tile([P, 1], F32, name="norm_rest")
        ws = sb.tile([P, I], F32, name="ws")
        nc.vector.scalar_tensor_tensor(
            part[:, lead], root[:, lead], 1.0, root[:, lead], ALU.mult, ALU.mult, accum_out=sum_lead[:]
        )
        nc.scalar.activation(part[:, rest], root[:, rest], ACT.Square, scale=512.0**-0.5, accum_out=sum_rest[:])
        nc.scalar.activation(
            norm_root[:], sum_lead[:], ACT.Abs_reciprocal_sqrt, bias=sum_rest[:], scale=1.0 / 512.0
        )
        for cols in (slice(0, FIRST), slice(FIRST, LEAD)):
            nc.vector.tensor_scalar(ws[:, cols], part[:, cols], norm_root[:], norm_root[:], ALU.mult, ALU.mult)
        nc.vector.tensor_scalar(norm_rest[:], norm_root[:], norm_root[:], 512.0, ALU.mult, ALU.mult)
        nc.scalar.activation(ws[:, rest], part[:, rest], ACT.Copy, scale=norm_rest[:])

        nc.vector.tensor_copy(f2[:].indirect(list3[:, : FIRST // 16]), ws[:, :FIRST])
        nc.vector.tensor_copy(f1[:].indirect(list1[:]), ws[:])
        nc.vector.tensor_copy(f2[:].indirect(list3[:, FIRST // 16 :]), ws[:, FIRST:])

        base_turned = sb.tile([P, T_PE], F32, name="base_turned")
        for k, n0 in enumerate(range(0, T_PE, N_MM)):
            bank = turned_banks[k]
            for j in range(blocks):
                nc.tensor.matmul(
                    bank[:, j * P : (j + 1) * P], f1[:, n0 + j * P : n0 + (j + 1) * P], ident[:],
                    start=False, stop=(j == blocks - 1), is_transpose=True,
                )
            nc.scalar.copy(base_turned[:, n0 : n0 + N_MM], bank[:])
        base_rest = sb.tile([P, T - T_PE], F32, name="base_rest")
        nc.gpsimd.tensor_tensor(base_rest[:], old_rest[:, T_PE - N_MM :], f1[:, T_PE:], ALU.add)

        result = sb.tile([P, T], F32, name="result")
        queues = [nc.sync, nc.scalar]
        for k, n0 in enumerate(range(0, T, N_MM)):
            cols = slice(n0, n0 + N_MM)
            if n0 < T_PE:
                bank = psum.tile([P, N_MM], F32, name="base_%d" % n0, tag="bank%d" % (2 + k))
                for j in range(blocks):
                    nc.tensor.transpose(
                        bank[:, j * P : (j + 1) * P], base_turned[:, n0 + j * P : n0 + (j + 1) * P], ident[:]
                    )
                base = bank[:]
            else:
                base = base_rest[:, n0 - T_PE : n0 - T_PE + N_MM]
            nc.vector.scalar_tensor_tensor(result[:, cols], f2[:, cols], share_col[:], base, ALU.mult, ALU.add)
            queues[k % 2].dma_start(out[:, cols], result[:, cols])
